import numpy as np
import ml_dtypes


def mxq(x, axis, fmt="e4m3"):
    dtype, down = {"e4m3": (ml_dtypes.float8_e4m3fn, 7), "e5m2": (ml_dtypes.float8_e5m2, 14)}[fmt]
    v = np.moveaxis(np.asarray(x, np.float32).astype(ml_dtypes.bfloat16).astype(np.float64), axis, -1)
    blocks = v.reshape(v.shape[:-1] + (-1, 32))
    amax = np.abs(blocks).max(-1, keepdims=True)
    byte = np.maximum(np.where(amax > 0, np.frexp(amax)[1] - 1 + 127, 0) - down, 1)
    scale = np.exp2(byte - 127.0)
    codes = (blocks / scale).astype(np.float32).astype(dtype).astype(np.float64)
    return np.moveaxis((codes * scale).reshape(v.shape), -1, axis)


WIDE = False


def mx_kscale(k):
    if not WIDE:
        return np.ones(k)
    levels = np.array([10, -10, 5, -5, 0])
    if k % 512:
        return np.exp2(np.random.permutation(np.resize(levels, k // 32))).repeat(32)
    a = np.empty((k // 512, 16))
    for p in range(k // 512):
        a[p, :8] = np.random.permutation(np.resize(levels, 8))
        for g in range(8):
            far = levels[np.abs(levels - a[p, g]) >= 10]
            a[p, g + 8] = far[np.random.randint(len(far))]
    return np.exp2(a.ravel()).repeat(32)


def f64(x):
    return np.asarray(x).astype(np.float64)


def striped(idx):
    return np.tile(np.asarray(idx).reshape(-1, 16).T, (8, 1)).astype(np.uint16)


def unstriped(offs):
    return offs[:16].T.reshape(-1).astype(np.int64)


E2M1 = np.array([0.0, 0.5, 1.0, 1.5, 2.0, 3.0, 4.0, 6.0, -0.0, -0.5, -1.0, -1.5, -2.0, -3.0, -4.0, -6.0])


def pack_weight(w, fmt):
    k, n = w.shape
    w = f64(np.asarray(w, np.float32).astype(ml_dtypes.bfloat16)).reshape(k // 32, 32, n)
    amax = np.abs(w).max(1)
    if fmt == "e4m3":
        byte = np.frexp(amax)[1] - 1 + 127 - 7
    else:
        mant, ex = np.frexp(amax / 6.0)
        byte = np.where(mant > 0.5, ex, ex - 1) + 127
    byte = np.clip(np.where(amax > 0, byte, 1), 1, 254)
    scaled = (w * np.exp2(127.0 - byte)[:, None, :]).reshape(k, n).astype(np.float32)
    by_word = np.ascontiguousarray(scaled.reshape(k // 512, 128, 4, n).transpose(0, 1, 3, 2))
    if fmt == "e4m3":
        words = by_word.astype(ml_dtypes.float8_e4m3fn).view(np.uint8)
    else:
        c = by_word.astype(ml_dtypes.float4_e2m1fn).view(np.uint8) & 0xF
        words = (c[..., 0::2] | (c[..., 1::2] << 4)).reshape(k // 512, 128, 2 * n)
    return np.ascontiguousarray(words), np.ascontiguousarray(byte.astype(np.uint8).reshape(k // 512, 16, n))


def unpack_weight(words, scales, fmt):
    g, _, n = scales.shape
    words = np.ascontiguousarray(words).reshape(g, 128, n, -1)
    if fmt == "e4m3":
        vals = words.view(ml_dtypes.float8_e4m3fn).astype(np.float64)
    else:
        nib = np.empty((g, 128, n, 4), np.uint8)
        nib[..., 0::2] = words & 0xF
        nib[..., 1::2] = words >> 4
        vals = E2M1[nib]
    vals = vals * np.repeat(np.exp2(scales.astype(np.float64) - 127.0), 8, axis=1)[..., None]
    return vals.transpose(0, 1, 3, 2).reshape(g * 512, n)


def bf(x):
    return np.asarray(x, np.float32).astype(ml_dtypes.bfloat16)


def planes(Y):
    r, m = Y.shape
    b = f64(bf(Y)).reshape(r // 32, 32, m)
    amax = np.abs(b).max(1)
    byte = np.clip(np.where(amax > 0, np.frexp(amax)[1] - 1 + 127 - 7, 1), 1, 254)
    codes = (b * np.exp2(127.0 - byte)[:, None, :]).reshape(r, m).astype(np.float32).astype(ml_dtypes.float8_e4m3fn).view(np.uint8)
    words = codes.reshape(r // 512, 128, 4, m).transpose(0, 1, 3, 2)
    return np.ascontiguousarray(words), np.ascontiguousarray(byte.astype(np.uint8).reshape(r // 512, 16, m))


K, T, J, N = 512, 512, 512, 512


def setup_inputs():
    n = np.random.standard_normal
    idx = np.random.randint(0, T, J)
    idx2 = np.random.randint(0, T, J)
    fk = mx_kscale(K)
    xtp = pack_weight(n((K, T)) / fk[:, None], "e4m3")
    wap = pack_weight(n((K, N)) * 1 / np.sqrt(K) * fk[:, None], "e2m1")
    return {
        "xt_words": xtp[0],
        "xt_scales": xtp[1],
        "wa_words": wap[0],
        "wa_scales": wap[1],
        "wb": (n((K, N)) * 1 / np.sqrt(K) * fk[:, None]).astype(np.float32),
        "offs": striped(idx),
        "offs2": striped(idx2),
    }


def reference(xt_words, xt_scales, wa_words, wa_scales, wb, offs, offs2):
    idx = unstriped(offs)
    idx2 = unstriped(offs2)
    xtu = unpack_weight(xt_words, xt_scales, "e4m3")
    wau = unpack_weight(wa_words, wa_scales, "e2m1")
    za = wau.T @ xtu
    wbq = mxq(f64(wb), 0, "e4m3")
    zb = wbq.T @ xtu
    m1 = np.maximum(za[:, idx], zb[:, idx2])
    d = np.abs(za[:, idx] - zb[:, idx2])
    y = m1 + np.log(1.0 + np.exp(0.0 - d))
    words, scales = planes(y)
    return y, words, scales

@@ -1,0 +1,239 @@
+from contextlib import ExitStack
+
+import concourse.mybir as mybir
+
+K, T, J, N = 512, 512, 512, 512
+FLOPS = 2 * 2 * K * N * T
+
+F32 = mybir.dt.float32
+BF16 = mybir.dt.bfloat16
+I32 = mybir.dt.int32
+U32 = mybir.dt.uint32
+U16 = mybir.dt.uint16
+U8 = mybir.dt.uint8
+FP8X4 = mybir.dt.float8_e4m3fn_x4
+FP4X4 = mybir.dt.float4_e2m1fn_x4
+ACT = mybir.ActivationFunctionType
+ALU = mybir.AluOpType
+
+P = 128
+PACK = 4
+HALF = J // 2
+CHUNK = 128
+CAP = 24.0
+
+
+def tile_list_smooth_larger_of_two_pl_kernel(
+    tc, xt_words, xt_scales, wa_words, wa_scales, wb, offs, offs2, out_0, out_1, out_2
+):
+    nc = tc.nc
+    with ExitStack() as ctx:
+        keep = ctx.enter_context(tc.tile_pool(name="keep", bufs=1))
+        psum = ctx.enter_context(tc.psum_pool(name="psum", bufs=1))
+
+        list_a = keep.tile([P, J // 16], U16, name="list_a")
+        list_b = keep.tile([P, J // 16], U16, name="list_b")
+        wa_raw = keep.tile([P, 2 * N], U8, name="wa_raw", align_bytes=64)
+        wa_raw_scales = keep.tile([P, N], U8, name="wa_raw_scales", align_bytes=64)
+        xt_codes = keep.tile([P, T], U32, name="xt_codes", align_bytes=64)
+        xt_plane = keep.tile([P, T], U8, name="xt_plane", align_bytes=64)
+        wb_raw = [keep.tile([P, PACK, N // 2], F32, name="wb_raw%d" % h) for h in range(2)]
+
+        for q in range(4):
+            nc.scalar.dma_start(
+                out=wa_raw_scales[32 * q : 32 * (q + 1), :].bitcast(I32),
+                in_=wa_scales[0, 4 * q : 4 * q + 4, :].bitcast(I32).partition_broadcast(8),
+            )
+        nc.sync.dma_start(out=wa_raw[:].bitcast(I32), in_=wa_words[0].bitcast(I32))
+        nc.sync.dma_start(
+            out=xt_codes[:].bitcast(I32), in_=xt_words[0].rearrange("p t r -> p (t r)").bitcast(I32)
+        )
+        for q in range(4):
+            nc.sync.dma_start(
+                out=xt_plane[32 * q : 32 * q + 4, :].bitcast(I32),
+                in_=xt_scales[0, 4 * q : 4 * q + 4, :].bitcast(I32),
+            )
+        wb_rows = wb.rearrange("(p i) n -> p i n", i=PACK)
+        nc.sync.dma_start(out=wb_raw[0][:], in_=wb_rows[:, :, 0 : N // 2])
+        nc.sync.dma_start(list_a[:], offs)
+        nc.sync.dma_start(out=wb_raw[1][:], in_=wb_rows[:, :, N // 2 : N])
+        nc.sync.dma_start(list_b[:], offs2)
+
+        wa_codes = keep.tile([P, 2 * N], U8, name="wa_codes", align_bytes=64)
+        wa_plane = keep.tile([P, N], U8, name="wa_plane", align_bytes=64)
+        nc.vector.tensor_copy(
+            out=wa_codes[:].bitcast(U16).rearrange("p (r m) -> p m r", r=PACK),
+            in_=wa_raw[:].bitcast(U16).rearrange("p (m r) -> p m r", r=PACK),
+        )
+        nc.vector.tensor_copy(
+            out=wa_plane[:].rearrange("p (r m) -> p m r", r=PACK),
+            in_=wa_raw_scales[:].rearrange("p (m r) -> p m r", r=PACK),
+        )
+
+        za_bank = [psum.tile([P, T], F32, name="za_bank%d" % r) for r in range(PACK)]
+        zb_bank = [psum.tile([P, T], F32, name="zb_bank%d" % r) for r in range(PACK)]
+        za = [keep.tile([P, T], F32, name="za%d" % r) for r in range(PACK)]
+        zb = [keep.tile([P, T], F32, name="zb%d" % r) for r in range(PACK)]
+        for r in range(PACK):
+            nc.tensor.matmul_mx(
+                out=za_bank[r][:],
+                lhsT=wa_codes[:, 2 * P * r : 2 * P * (r + 1)].bitcast(FP4X4),
+                lhsT_scale=wa_plane[:, P * r : P * (r + 1)],
+                rhs=xt_codes[:].bitcast(FP8X4),
+                rhs_scale=xt_plane[:],
+                start=True,
+                stop=True,
+            )
+
+        picked_a = keep.tile([P, PACK, J], F32, name="picked_a")
+        gap = keep.tile([P, PACK, J], F32, name="gap")
+        capped = keep.tile([P, PACK, J], F32, name="capped")
+        grown = keep.tile([P, PACK, J], F32, name="grown")
+        base = keep.tile([P, PACK, J], F32, name="base")
+        y = keep.tile([P, PACK, J], F32, name="y")
+
+        def entries(lst, h):
+            return lst[:, h * HALF // 16 : (h + 1) * HALF // 16]
+
+        def slots(h):
+            return slice(h * HALF, (h + 1) * HALF)
+
+        def pick_a(r):
+            for h in range(2):
+                nc.scalar.activation(out=picked_a[:, r, slots(h)], in_=za[r][:].indirect(entries(list_a, h)), func=ACT.Copy)
+
+        def empty_on_scalar(dst, bank):
+            nc.scalar.activation(out=dst[:], in_=bank[:], func=ACT.Copy)
+
+        def empty_on_vector(dst, bank):
+            nc.vector.tensor_copy(out=dst[:], in_=bank[:])
+
+        wb_bf = keep.tile([P, PACK, P, PACK], BF16, name="wb_bf", align_bytes=64)
+        wb_codes = keep.tile([P, N], U32, name="wb_codes", align_bytes=64)
+        wb_plane = keep.tile([P, N], U8, name="wb_plane", align_bytes=64)
+
+        def round_wb(h):
+            nc.vector.tensor_copy(
+                out=wb_bf[:, :, h * P // 2 : (h + 1) * P // 2, :].rearrange("p r m i -> p m i r"),
+                in_=wb_raw[h][:].rearrange("p i (m r) -> p m i r", r=PACK),
+            )
+
+        empty_on_scalar(za[0], za_bank[0])
+        round_wb(0)
+        empty_on_vector(za[1], za_bank[1])
+        pick_a(0)
+        round_wb(1)
+        pick_a(1)
+        for r in range(PACK):
+            cols = slice(P * r, P * (r + 1))
+            nc.vector.quantize_mx(
+                out=wb_codes[:, cols].bitcast(FP8X4),
+                scales=wb_plane[:, cols],
+                in_=wb_bf[:, r, :, :].rearrange("p m i -> p (m i)"),
+            )
+            nc.tensor.matmul_mx(
+                out=zb_bank[r][:],
+                lhsT=wb_codes[:, cols].bitcast(FP8X4),
+                lhsT_scale=wb_plane[:, cols],
+                rhs=xt_codes[:].bitcast(FP8X4),
+                rhs_scale=xt_plane[:],
+                start=True,
+                stop=True,
+            )
+
+        def pick_b(r):
+            for h in range(2):
+                nc.vector.tensor_tensor(
+                    out=gap[:, r, slots(h)],
+                    in0=zb[r][:].indirect(entries(list_b, h)),
+                    in1=picked_a[:, r, slots(h)],
+                    op=ALU.subtract,
+                )
+
+        def cap(r, cols):
+            nc.vector.tensor_scalar_min(out=capped[:, r, cols], in0=gap[:, r, cols], scalar1=CAP)
+
+        def grow(r, cols):
+            nc.scalar.activation(out=grown[:, r, cols], in_=capped[:, r, cols], func=ACT.Exp)
+
+        every = slice(0, J)
+        empty_on_vector(zb[0], zb_bank[0])
+        empty_on_scalar(za[2], za_bank[2])
+        pick_b(0)
+        pick_a(2)
+        empty_on_vector(zb[1], zb_bank[1])
+        empty_on_scalar(zb[2], zb_bank[2])
+        pick_b(1)
+        cap(0, every)
+        empty_on_scalar(za[3], za_bank[3])
+        pick_a(3)
+        pick_b(2)
+        cap(1, every)
+        empty_on_scalar(zb[3], zb_bank[3])
+        grow(0, every)
+        grow(1, every)
+        cap(2, every)
+        pick_b(3)
+        grow(2, every)
+        for h in range(2):
+            cap(3, slots(h))
+            grow(3, slots(h))
+
+        for h in range(2):
+            nc.vector.scalar_tensor_tensor(
+                out=base[:, :, slots(h)], in0=gap[:, :, slots(h)], scalar=CAP, in1=picked_a[:, :, slots(h)], op0=ALU.max, op1=ALU.add
+            )
+
+        chunks = J // CHUNK
+        y_rows = out_0.rearrange("(p r) j -> p r j", r=PACK)
+        y_codes = keep.tile([P, J], U32, name="y_codes", align_bytes=64)
+        y_plane = keep.tile([P, J], U8, name="y_plane", align_bytes=64)
+        y_bf = [keep.tile([P, CHUNK, PACK], BF16, name="y_bf%d" % c, align_bytes=64) for c in range(chunks)]
+        word_rows = out_1[0].rearrange("p j r -> p (j r)").bitcast(I32)
+
+        def span(c):
+            return slice(c * CHUNK, (c + 1) * CHUNK)
+
+        def finish(c):
+            soft = capped[:, :, span((c + chunks // 2) % chunks)]
+            nc.scalar.activation(out=soft, in_=grown[:, :, span(c)], func=ACT.Ln, bias=1.0)
+            nc.vector.scalar_tensor_tensor(
+                out=y[:, :, span(c)], in0=soft, scalar=-CAP, in1=base[:, :, span(c)], op0=ALU.add, op1=ALU.add
+            )
+            nc.sync.dma_start(out=y_rows[:, :, span(c)], in_=y[:, :, span(c)])
+
+        def round_y(c):
+            dst = y_bf[c][:].rearrange("p (g i) r -> p g r i", i=4)
+            src = y[:, :, span(c)].rearrange("p r (g i) -> p g r i", i=4)
+            if c == 2:
+                nc.scalar.copy(out=dst, in_=src)
+            else:
+                nc.vector.tensor_copy(out=dst, in_=src)
+
+        def quantize_y(c):
+            nc.vector.quantize_mx(
+                out=y_codes[:, span(c)].bitcast(FP8X4),
+                scales=y_plane[:, span(c)],
+                in_=y_bf[c][:].rearrange("p j r -> p (j r)"),
+            )
+
+        finish(0)
+        finish(1)
+        round_y(0)
+        finish(2)
+        round_y(1)
+        quantize_y(0)
+        finish(3)
+        round_y(2)
+        quantize_y(1)
+        nc.sync.dma_start(out=word_rows[:, 0:HALF], in_=y_codes[:, 0:HALF].bitcast(I32))
+        round_y(3)
+        quantize_y(2)
+        quantize_y(3)
+        nc.sync.dma_start(out=word_rows[:, HALF:J], in_=y_codes[:, HALF:J].bitcast(I32))
+        for q in range(4):
+            queue = nc.sync if q % 2 else nc.scalar
+            queue.dma_start(
+                out=out_2[0, 4 * q : 4 * q + 4, :].bitcast(I32),
+                in_=y_plane[32 * q : 32 * q + 4, :].bitcast(I32),
+            )

@@ -37,7 +37,8 @@ def tile_list_smooth_larger_of_two_pl_kernel(
         wa_raw_scales = keep.tile([P, N], U8, name="wa_raw_scales", align_bytes=64)
         xt_codes = keep.tile([P, T], U32, name="xt_codes", align_bytes=64)
         xt_plane = keep.tile([P, T], U8, name="xt_plane", align_bytes=64)
-        wb_raw = [keep.tile([P, PACK, N // 2], F32, name="wb_raw%d" % h) for h in range(2)]
+        picked_a = keep.tile([P, PACK, J], F32, name="picked_a")
+        wb_raw = [keep.tile([P, PACK, N // 2], F32, name="wb_raw%d" % h)[:] for h in range(2)]
 
         for q in range(4):
             nc.scalar.dma_start(
@@ -53,10 +54,10 @@ def tile_list_smooth_larger_of_two_pl_kernel(
                 out=xt_plane[32 * q : 32 * q + 4, :].bitcast(I32),
                 in_=xt_scales[0, 4 * q : 4 * q + 4, :].bitcast(I32),
             )
-        wb_rows = wb.rearrange("(p i) n -> p i n", i=PACK)
-        nc.sync.dma_start(out=wb_raw[0][:], in_=wb_rows[:, :, 0 : N // 2])
         nc.sync.dma_start(list_a[:], offs)
-        nc.sync.dma_start(out=wb_raw[1][:], in_=wb_rows[:, :, N // 2 : N])
+        wb_rows = wb.rearrange("(p i) n -> p i n", i=PACK)
+        nc.sync.dma_start(out=wb_raw[0], in_=wb_rows[:, :, 0 : N // 2])
+        nc.sync.dma_start(out=wb_raw[1], in_=wb_rows[:, :, N // 2 : N])
         nc.sync.dma_start(list_b[:], offs2)
 
         wa_codes = keep.tile([P, 2 * N], U8, name="wa_codes", align_bytes=64)
@@ -70,22 +71,30 @@ def tile_list_smooth_larger_of_two_pl_kernel(
             in_=wa_raw_scales[:].rearrange("p (m r) -> p m r", r=PACK),
         )
 
-        za_bank = [psum.tile([P, T], F32, name="za_bank%d" % r) for r in range(PACK)]
         zb_bank = [psum.tile([P, T], F32, name="zb_bank%d" % r) for r in range(PACK)]
+        za_bank = [psum.tile([P, T], F32, name="za_bank%d" % r) for r in range(PACK - 1)] + [zb_bank[1]]
+        spare_bank = psum.tile([P, T], F32, name="spare_bank")
         za = [keep.tile([P, T], F32, name="za%d" % r) for r in range(PACK)]
         zb = [keep.tile([P, T], F32, name="zb%d" % r) for r in range(PACK)]
-        for r in range(PACK):
+
+        def multiply_a(r, bank, tokens):
             nc.tensor.matmul_mx(
-                out=za_bank[r][:],
+                out=bank[:, tokens],
                 lhsT=wa_codes[:, 2 * P * r : 2 * P * (r + 1)].bitcast(FP4X4),
                 lhsT_scale=wa_plane[:, P * r : P * (r + 1)],
-                rhs=xt_codes[:].bitcast(FP8X4),
-                rhs_scale=xt_plane[:],
+                rhs=xt_codes[:, tokens].bitcast(FP8X4),
+                rhs_scale=xt_plane[:, tokens],
                 start=True,
                 stop=True,
             )
 
-        picked_a = keep.tile([P, PACK, J], F32, name="picked_a")
+        every = slice(0, J)
+        low, high = slice(0, T // 2), slice(T // 2, T)
+        multiply_a(0, za_bank[0], low)
+        multiply_a(0, spare_bank, high)
+        multiply_a(1, za_bank[1], every)
+        multiply_a(2, za_bank[2], every)
+
         gap = keep.tile([P, PACK, J], F32, name="gap")
         capped = keep.tile([P, PACK, J], F32, name="capped")
         grown = keep.tile([P, PACK, J], F32, name="grown")
@@ -103,10 +112,10 @@ def tile_list_smooth_larger_of_two_pl_kernel(
                 nc.scalar.activation(out=picked_a[:, r, slots(h)], in_=za[r][:].indirect(entries(list_a, h)), func=ACT.Copy)
 
         def empty_on_scalar(dst, bank):
-            nc.scalar.activation(out=dst[:], in_=bank[:], func=ACT.Copy)
+            nc.scalar.activation(out=dst, in_=bank, func=ACT.Copy)
 
         def empty_on_vector(dst, bank):
-            nc.vector.tensor_copy(out=dst[:], in_=bank[:])
+            nc.vector.tensor_copy(out=dst, in_=bank)
 
         wb_bf = keep.tile([P, PACK, P, PACK], BF16, name="wb_bf", align_bytes=64)
         wb_codes = keep.tile([P, N], U32, name="wb_codes", align_bytes=64)
@@ -115,13 +124,14 @@ def tile_list_smooth_larger_of_two_pl_kernel(
         def round_wb(h):
             nc.vector.tensor_copy(
                 out=wb_bf[:, :, h * P // 2 : (h + 1) * P // 2, :].rearrange("p r m i -> p m i r"),
-                in_=wb_raw[h][:].rearrange("p i (m r) -> p m i r", r=PACK),
+                in_=wb_raw[h].rearrange("p i (m r) -> p m i r", r=PACK),
             )
 
-        empty_on_scalar(za[0], za_bank[0])
-        round_wb(0)
-        empty_on_vector(za[1], za_bank[1])
+        empty_on_scalar(za[0][:, low], za_bank[0][:, low])
+        empty_on_vector(za[0][:, high], spare_bank[:, high])
         pick_a(0)
+        empty_on_scalar(za[1][:], za_bank[1][:])
+        round_wb(0)
         round_wb(1)
         pick_a(1)
         for r in range(PACK):
@@ -156,20 +166,20 @@ def tile_list_smooth_larger_of_two_pl_kernel(
         def grow(r, cols):
             nc.scalar.activation(out=grown[:, r, cols], in_=capped[:, r, cols], func=ACT.Exp)
 
-        every = slice(0, J)
-        empty_on_vector(zb[0], zb_bank[0])
-        empty_on_scalar(za[2], za_bank[2])
-        pick_b(0)
+        empty_on_vector(za[2][:], za_bank[2][:])
         pick_a(2)
-        empty_on_vector(zb[1], zb_bank[1])
-        empty_on_scalar(zb[2], zb_bank[2])
+        empty_on_vector(zb[0][:], zb_bank[0][:])
+        empty_on_scalar(zb[1][:], zb_bank[1][:])
+        multiply_a(3, za_bank[3], every)
+        empty_on_scalar(zb[2][:], zb_bank[2][:])
+        empty_on_scalar(za[3][:], za_bank[3][:])
+        pick_a(3)
+        empty_on_scalar(zb[3][:], zb_bank[3][:])
+        pick_b(0)
         pick_b(1)
         cap(0, every)
-        empty_on_scalar(za[3], za_bank[3])
-        pick_a(3)
         pick_b(2)
         cap(1, every)
-        empty_on_scalar(zb[3], zb_bank[3])
         grow(0, every)
         grow(1, every)
         cap(2, every)
@@ -179,10 +189,7 @@ def tile_list_smooth_larger_of_two_pl_kernel(
             cap(3, slots(h))
             grow(3, slots(h))
 
-        for h in range(2):
-            nc.vector.scalar_tensor_tensor(
-                out=base[:, :, slots(h)], in0=gap[:, :, slots(h)], scalar=CAP, in1=picked_a[:, :, slots(h)], op0=ALU.max, op1=ALU.add
-            )
+        nc.vector.scalar_tensor_tensor(out=base[:], in0=gap[:], scalar=CAP, in1=picked_a[:], op0=ALU.max, op1=ALU.add)
 
         chunks = J // CHUNK
         y_rows = out_0.rearrange("(p r) j -> p r j", r=PACK)
@@ -205,7 +212,7 @@ def tile_list_smooth_larger_of_two_pl_kernel(
         def round_y(c):
             dst = y_bf[c][:].rearrange("p (g i) r -> p g r i", i=4)
             src = y[:, :, span(c)].rearrange("p r (g i) -> p g r i", i=4)
-            if c == 2:
+            if c in (1, 2):
                 nc.scalar.copy(out=dst, in_=src)
             else:
                 nc.vector.tensor_copy(out=dst, in_=src)
@@ -221,9 +228,9 @@ def tile_list_smooth_larger_of_two_pl_kernel(
         finish(1)
         round_y(0)
         finish(2)
-        round_y(1)
         quantize_y(0)
         finish(3)
+        round_y(1)
         round_y(2)
         quantize_y(1)
         nc.sync.dma_start(out=word_rows[:, 0:HALF], in_=y_codes[:, 0:HALF].bitcast(I32))

@@ -45,15 +45,21 @@ def tile_list_smooth_larger_of_two_pl_kernel(
                 out=wa_raw_scales[32 * q : 32 * (q + 1), :].bitcast(I32),
                 in_=wa_scales[0, 4 * q : 4 * q + 4, :].bitcast(I32).partition_broadcast(8),
             )
-        nc.sync.dma_start(out=wa_raw[:].bitcast(I32), in_=wa_words[0].bitcast(I32))
-        nc.sync.dma_start(
-            out=xt_codes[:].bitcast(I32), in_=xt_words[0].rearrange("p t r -> p (t r)").bitcast(I32)
-        )
-        for q in range(4):
+
+        def load_xt_scales(q):
             nc.sync.dma_start(
                 out=xt_plane[32 * q : 32 * q + 4, :].bitcast(I32),
                 in_=xt_scales[0, 4 * q : 4 * q + 4, :].bitcast(I32),
             )
+
+        load_xt_scales(0)
+        load_xt_scales(1)
+        nc.sync.dma_start(out=wa_raw[:].bitcast(I32), in_=wa_words[0].bitcast(I32))
+        nc.sync.dma_start(
+            out=xt_codes[:].bitcast(I32), in_=xt_words[0].rearrange("p t r -> p (t r)").bitcast(I32)
+        )
+        load_xt_scales(2)
+        load_xt_scales(3)
         nc.sync.dma_start(list_a[:], offs)
         wb_rows = wb.rearrange("(p i) n -> p i n", i=PACK)
         nc.sync.dma_start(out=wb_raw[0], in_=wb_rows[:, :, 0 : N // 2])
@@ -167,9 +173,9 @@ def tile_list_smooth_larger_of_two_pl_kernel(
             nc.scalar.activation(out=grown[:, r, cols], in_=capped[:, r, cols], func=ACT.Exp)
 
         empty_on_vector(za[2][:], za_bank[2][:])
-        pick_a(2)
         empty_on_vector(zb[0][:], zb_bank[0][:])
         empty_on_scalar(zb[1][:], zb_bank[1][:])
+        pick_a(2)
         multiply_a(3, za_bank[3], every)
         empty_on_scalar(zb[2][:], zb_bank[2][:])
         empty_on_scalar(za[3][:], za_bank[3][:])
@@ -201,12 +207,16 @@ def tile_list_smooth_larger_of_two_pl_kernel(
         def span(c):
             return slice(c * CHUNK, (c + 1) * CHUNK)
 
-        def finish(c):
-            soft = capped[:, :, span((c + chunks // 2) % chunks)]
-            nc.scalar.activation(out=soft, in_=grown[:, :, span(c)], func=ACT.Ln, bias=1.0)
+        def finish(first, width):
+            cols = slice(first, first + width)
+            moved = (first + HALF) % J
+            soft = capped[:, :, moved : moved + width]
+            nc.scalar.activation(out=soft, in_=grown[:, :, cols], func=ACT.Ln, bias=1.0)
             nc.vector.scalar_tensor_tensor(
-                out=y[:, :, span(c)], in0=soft, scalar=-CAP, in1=base[:, :, span(c)], op0=ALU.add, op1=ALU.add
+                out=y[:, :, cols], in0=soft, scalar=-CAP, in1=base[:, :, cols], op0=ALU.add, op1=ALU.add
             )
+
+        def store_y(c):
             nc.sync.dma_start(out=y_rows[:, :, span(c)], in_=y[:, :, span(c)])
 
         def round_y(c):
@@ -224,12 +234,17 @@ def tile_list_smooth_larger_of_two_pl_kernel(
                 in_=y_bf[c][:].rearrange("p j r -> p (j r)"),
             )
 
-        finish(0)
-        finish(1)
+        finish(0, CHUNK // 2)
+        finish(CHUNK // 2, CHUNK // 2)
+        store_y(0)
+        finish(1 * CHUNK, CHUNK)
+        store_y(1)
         round_y(0)
-        finish(2)
+        finish(2 * CHUNK, CHUNK)
+        store_y(2)
         quantize_y(0)
-        finish(3)
+        finish(3 * CHUNK, CHUNK)
+        store_y(3)
         round_y(1)
         round_y(2)
         quantize_y(1)

from contextlib import ExitStack

import concourse.mybir as mybir

K, T, J, N = 512, 512, 512, 512
FLOPS = 2 * 2 * K * N * T

F32 = mybir.dt.float32
BF16 = mybir.dt.bfloat16
I32 = mybir.dt.int32
U32 = mybir.dt.uint32
U16 = mybir.dt.uint16
U8 = mybir.dt.uint8
FP8X4 = mybir.dt.float8_e4m3fn_x4
FP4X4 = mybir.dt.float4_e2m1fn_x4
ACT = mybir.ActivationFunctionType
ALU = mybir.AluOpType

P = 128
PACK = 4
HALF = J // 2
CHUNK = 128
CAP = 24.0


def tile_list_smooth_larger_of_two_pl_kernel(
    tc, xt_words, xt_scales, wa_words, wa_scales, wb, offs, offs2, out_0, out_1, out_2
):
    nc = tc.nc
    with ExitStack() as ctx:
        keep = ctx.enter_context(tc.tile_pool(name="keep", bufs=1))
        psum = ctx.enter_context(tc.psum_pool(name="psum", bufs=1))

        list_a = keep.tile([P, J // 16], U16, name="list_a")
        list_b = keep.tile([P, J // 16], U16, name="list_b")
        wa_raw = keep.tile([P, 2 * N], U8, name="wa_raw", align_bytes=64)
        wa_raw_scales = keep.tile([P, N], U8, name="wa_raw_scales", align_bytes=64)
        xt_codes = keep.tile([P, T], U32, name="xt_codes", align_bytes=64)
        xt_plane = keep.tile([P, T], U8, name="xt_plane", align_bytes=64)
        picked_a = keep.tile([P, PACK, J], F32, name="picked_a")
        wb_raw = [keep.tile([P, PACK, N // 2], F32, name="wb_raw%d" % h)[:] for h in range(2)]

        for q in range(4):
            nc.scalar.dma_start(
                out=wa_raw_scales[32 * q : 32 * (q + 1), :].bitcast(I32),
                in_=wa_scales[0, 4 * q : 4 * q + 4, :].bitcast(I32).partition_broadcast(8),
            )

        def load_xt_scales(q):
            nc.sync.dma_start(
                out=xt_plane[32 * q : 32 * q + 4, :].bitcast(I32),
                in_=xt_scales[0, 4 * q : 4 * q + 4, :].bitcast(I32),
            )

        load_xt_scales(0)
        load_xt_scales(1)
        nc.sync.dma_start(out=wa_raw[:].bitcast(I32), in_=wa_words[0].bitcast(I32))
        nc.sync.dma_start(
            out=xt_codes[:].bitcast(I32), in_=xt_words[0].rearrange("p t r -> p (t r)").bitcast(I32)
        )
        load_xt_scales(2)
        load_xt_scales(3)
        nc.sync.dma_start(list_a[:], offs)
        wb_rows = wb.rearrange("(p i) n -> p i n", i=PACK)
        nc.sync.dma_start(out=wb_raw[0], in_=wb_rows[:, :, 0 : N // 2])
        nc.sync.dma_start(out=wb_raw[1], in_=wb_rows[:, :, N // 2 : N])
        nc.sync.dma_start(list_b[:], offs2)

        wa_codes = keep.tile([P, 2 * N], U8, name="wa_codes", align_bytes=64)
        wa_plane = keep.tile([P, N], U8, name="wa_plane", align_bytes=64)
        nc.vector.tensor_copy(
            out=wa_codes[:].bitcast(U16).rearrange("p (r m) -> p m r", r=PACK),
            in_=wa_raw[:].bitcast(U16).rearrange("p (m r) -> p m r", r=PACK),
        )
        nc.vector.tensor_copy(
            out=wa_plane[:].rearrange("p (r m) -> p m r", r=PACK),
            in_=wa_raw_scales[:].rearrange("p (m r) -> p m r", r=PACK),
        )

        zb_bank = [psum.tile([P, T], F32, name="zb_bank%d" % r) for r in range(PACK)]
        za_bank = [psum.tile([P, T], F32, name="za_bank%d" % r) for r in range(PACK - 1)] + [zb_bank[1]]
        spare_bank = psum.tile([P, T], F32, name="spare_bank")
        za = [keep.tile([P, T], F32, name="za%d" % r) for r in range(PACK)]
        zb = [keep.tile([P, T], F32, name="zb%d" % r) for r in range(PACK)]

        def multiply_a(r, bank, tokens):
            nc.tensor.matmul_mx(
                out=bank[:, tokens],
                lhsT=wa_codes[:, 2 * P * r : 2 * P * (r + 1)].bitcast(FP4X4),
                lhsT_scale=wa_plane[:, P * r : P * (r + 1)],
                rhs=xt_codes[:, tokens].bitcast(FP8X4),
                rhs_scale=xt_plane[:, tokens],
                start=True,
                stop=True,
            )

        every = slice(0, J)
        low, high = slice(0, T // 2), slice(T // 2, T)
        multiply_a(0, za_bank[0], low)
        multiply_a(0, spare_bank, high)
        multiply_a(1, za_bank[1], every)
        multiply_a(2, za_bank[2], every)

        gap = keep.tile([P, PACK, J], F32, name="gap")
        capped = keep.tile([P, PACK, J], F32, name="capped")
        grown = keep.tile([P, PACK, J], F32, name="grown")
        base = keep.tile([P, PACK, J], F32, name="base")
        y = keep.tile([P, PACK, J], F32, name="y")

        def entries(lst, h):
            return lst[:, h * HALF // 16 : (h + 1) * HALF // 16]

        def slots(h):
            return slice(h * HALF, (h + 1) * HALF)

        def pick_a(r):
            for h in range(2):
                nc.scalar.activation(out=picked_a[:, r, slots(h)], in_=za[r][:].indirect(entries(list_a, h)), func=ACT.Copy)

        def empty_on_scalar(dst, bank):
            nc.scalar.activation(out=dst, in_=bank, func=ACT.Copy)

        def empty_on_vector(dst, bank):
            nc.vector.tensor_copy(out=dst, in_=bank)

        wb_bf = keep.tile([P, PACK, P, PACK], BF16, name="wb_bf", align_bytes=64)
        wb_codes = keep.tile([P, N], U32, name="wb_codes", align_bytes=64)
        wb_plane = keep.tile([P, N], U8, name="wb_plane", align_bytes=64)

        def round_wb(h):
            nc.vector.tensor_copy(
                out=wb_bf[:, :, h * P // 2 : (h + 1) * P // 2, :].rearrange("p r m i -> p m i r"),
                in_=wb_raw[h].rearrange("p i (m r) -> p m i r", r=PACK),
            )

        empty_on_scalar(za[0][:, low], za_bank[0][:, low])
        empty_on_vector(za[0][:, high], spare_bank[:, high])
        pick_a(0)
        empty_on_scalar(za[1][:], za_bank[1][:])
        round_wb(0)
        round_wb(1)
        pick_a(1)
        for r in range(PACK):
            cols = slice(P * r, P * (r + 1))
            nc.vector.quantize_mx(
                out=wb_codes[:, cols].bitcast(FP8X4),
                scales=wb_plane[:, cols],
                in_=wb_bf[:, r, :, :].rearrange("p m i -> p (m i)"),
            )
            nc.tensor.matmul_mx(
                out=zb_bank[r][:],
                lhsT=wb_codes[:, cols].bitcast(FP8X4),
                lhsT_scale=wb_plane[:, cols],
                rhs=xt_codes[:].bitcast(FP8X4),
                rhs_scale=xt_plane[:],
                start=True,
                stop=True,
            )

        def pick_b(r):
            for h in range(2):
                nc.vector.tensor_tensor(
                    out=gap[:, r, slots(h)],
                    in0=zb[r][:].indirect(entries(list_b, h)),
                    in1=picked_a[:, r, slots(h)],
                    op=ALU.subtract,
                )

        def cap(r, cols):
            nc.vector.tensor_scalar_min(out=capped[:, r, cols], in0=gap[:, r, cols], scalar1=CAP)

        def grow(r, cols):
            nc.scalar.activation(out=grown[:, r, cols], in_=capped[:, r, cols], func=ACT.Exp)

        empty_on_vector(za[2][:], za_bank[2][:])
        empty_on_vector(zb[0][:], zb_bank[0][:])
        empty_on_scalar(zb[1][:], zb_bank[1][:])
        pick_a(2)
        multiply_a(3, za_bank[3], every)
        empty_on_scalar(zb[2][:], zb_bank[2][:])
        empty_on_scalar(za[3][:], za_bank[3][:])
        pick_a(3)
        empty_on_scalar(zb[3][:], zb_bank[3][:])
        pick_b(0)
        pick_b(1)
        cap(0, every)
        pick_b(2)
        cap(1, every)
        grow(0, every)
        grow(1, every)
        cap(2, every)
        pick_b(3)
        grow(2, every)
        for h in range(2):
            cap(3, slots(h))
            grow(3, slots(h))

        nc.vector.scalar_tensor_tensor(out=base[:], in0=gap[:], scalar=CAP, in1=picked_a[:], op0=ALU.max, op1=ALU.add)

        chunks = J // CHUNK
        y_rows = out_0.rearrange("(p r) j -> p r j", r=PACK)
        y_codes = keep.tile([P, J], U32, name="y_codes", align_bytes=64)
        y_plane = keep.tile([P, J], U8, name="y_plane", align_bytes=64)
        y_bf = [keep.tile([P, CHUNK, PACK], BF16, name="y_bf%d" % c, align_bytes=64) for c in range(chunks)]
        word_rows = out_1[0].rearrange("p j r -> p (j r)").bitcast(I32)

        def span(c):
            return slice(c * CHUNK, (c + 1) * CHUNK)

        def finish(first, width):
            cols = slice(first, first + width)
            moved = (first + HALF) % J
            soft = capped[:, :, moved : moved + width]
            nc.scalar.activation(out=soft, in_=grown[:, :, cols], func=ACT.Ln, bias=1.0)
            nc.vector.scalar_tensor_tensor(
                out=y[:, :, cols], in0=soft, scalar=-CAP, in1=base[:, :, cols], op0=ALU.add, op1=ALU.add
            )

        def store_y(c):
            nc.sync.dma_start(out=y_rows[:, :, span(c)], in_=y[:, :, span(c)])

        def round_y(c):
            dst = y_bf[c][:].rearrange("p (g i) r -> p g r i", i=4)
            src = y[:, :, span(c)].rearrange("p r (g i) -> p g r i", i=4)
            if c in (1, 2):
                nc.scalar.copy(out=dst, in_=src)
            else:
                nc.vector.tensor_copy(out=dst, in_=src)

        def quantize_y(c):
            nc.vector.quantize_mx(
                out=y_codes[:, span(c)].bitcast(FP8X4),
                scales=y_plane[:, span(c)],
                in_=y_bf[c][:].rearrange("p j r -> p (j r)"),
            )

        finish(0, CHUNK // 2)
        finish(CHUNK // 2, CHUNK // 2)
        store_y(0)
        finish(1 * CHUNK, CHUNK)
        store_y(1)
        round_y(0)
        finish(2 * CHUNK, CHUNK)
        store_y(2)
        quantize_y(0)
        finish(3 * CHUNK, CHUNK)
        store_y(3)
        round_y(1)
        round_y(2)
        quantize_y(1)
        nc.sync.dma_start(out=word_rows[:, 0:HALF], in_=y_codes[:, 0:HALF].bitcast(I32))
        round_y(3)
        quantize_y(2)
        quantize_y(3)
        nc.sync.dma_start(out=word_rows[:, HALF:J], in_=y_codes[:, HALF:J].bitcast(I32))
        for q in range(4):
            queue = nc.sync if q % 2 else nc.scalar
            queue.dma_start(
                out=out_2[0, 4 * q : 4 * q + 4, :].bitcast(I32),
                in_=y_plane[32 * q : 32 * q + 4, :].bitcast(I32),
            )
